import numpy as np
import ml_dtypes


def mxq(x, axis, fmt="e4m3"):
    dtype, down = {"e4m3": (ml_dtypes.float8_e4m3fn, 7), "e5m2": (ml_dtypes.float8_e5m2, 14)}[fmt]
    v = np.moveaxis(np.asarray(x, np.float32).astype(ml_dtypes.bfloat16).astype(np.float64), axis, -1)
    blocks = v.reshape(v.shape[:-1] + (-1, 32))
    amax = np.abs(blocks).max(-1, keepdims=True)
    byte = np.maximum(np.where(amax > 0, np.frexp(amax)[1] - 1 + 127, 0) - down, 1)
    scale = np.exp2(byte - 127.0)
    codes = (blocks / scale).astype(np.float32).astype(dtype).astype(np.float64)
    return np.moveaxis((codes * scale).reshape(v.shape), -1, axis)


WIDE = False


def mx_kscale(k):
    if not WIDE:
        return np.ones(k)
    levels = np.array([10, -10, 5, -5, 0])
    if k % 512:
        return np.exp2(np.random.permutation(np.resize(levels, k // 32))).repeat(32)
    a = np.empty((k // 512, 16))
    for p in range(k // 512):
        a[p, :8] = np.random.permutation(np.resize(levels, 8))
        for g in range(8):
            far = levels[np.abs(levels - a[p, g]) >= 10]
            a[p, g + 8] = far[np.random.randint(len(far))]
    return np.exp2(a.ravel()).repeat(32)


def f64(x):
    return np.asarray(x).astype(np.float64)


def striped(idx):
    return np.tile(idx.reshape(-1, 16).T, (8, 1)).astype(np.uint16)


def unstriped(offs):
    return offs[:16].T.reshape(-1).astype(np.int64)


def striped8(idx):
    return np.concatenate([x.reshape(-1, 16).T for x in idx]).astype(np.uint16)


def runs(offs, k):
    lists = np.stack([offs[16 * r : 16 * r + 16].T.reshape(-1) for r in range(8)]).astype(np.int64)
    return lists[np.arange(k) % 512 // 64]


def pack_weight(w):
    k, n = w.shape
    w = f64(np.asarray(w, np.float32).astype(ml_dtypes.bfloat16)).reshape(k // 32, 32, n)
    amax = np.abs(w).max(1)
    byte = np.clip(np.where(amax > 0, np.frexp(amax)[1] - 1 + 127 - 7, 1), 1, 254)
    scaled = (w * np.exp2(127.0 - byte)[:, None, :]).reshape(k, n).astype(np.float32)
    words = np.ascontiguousarray(scaled.reshape(k // 512, 128, 4, n).transpose(0, 1, 3, 2)).astype(ml_dtypes.float8_e4m3fn).view(np.uint8)
    return words, np.ascontiguousarray(byte.astype(np.uint8).reshape(k // 512, 16, n))


def unpack_weight(words, scales):
    g, p, n, _ = words.shape
    vals = np.ascontiguousarray(words).view(ml_dtypes.float8_e4m3fn).astype(np.float64) * np.repeat(np.exp2(scales.astype(np.float64) - 127.0), 8, axis=1)[..., None]
    return vals.transpose(0, 1, 3, 2).reshape(g * 512, n)


K, T, S, N, H, G, W = 512, 2048, 512, 512, 512, 2048, 256


def setup_inputs():
    n = np.random.standard_normal
    s = mx_kscale(K)[:, None]
    u = mx_kscale(S)
    packed_xT = pack_weight(n((K, T)) * s)
    packed_dT = pack_weight(n((K, G)) / s)
    perm = np.random.permutation(S)
    return {
        "x_words": packed_xT[0],
        "x_scales": packed_xT[1],
        "w1": (n((K, H)) / np.sqrt(K) / s).astype(np.float32),
        "d_words": packed_dT[0],
        "d_scales": packed_dT[1],
        "gn": (np.random.uniform(0.5, 1.5, (H, 1)) * u[:, None]).astype(np.float32),
        "w2": (n((H, N)) / np.sqrt(H) / u[:, None]).astype(np.float32),
        "offs": striped(np.random.permutation(T)[:S]),
        "k1": striped8(np.random.randint(0, G, (8, H))),
        "two": striped(np.random.permutation(T)[:S]),
        "n1": striped(np.random.permutation(S)),
        "n2": striped(np.random.permutation(S)),
        "n3": striped(perm[:W]),
        "n4": striped(perm[W:]),
    }


def reference(x_words, x_scales, w1, d_words, d_scales, gn, w2, offs, k1, two, n1, n2, n3, n4):
    xq = unpack_weight(x_words, x_scales)[:, unstriped(offs)]
    y = mxq(f64(w1), 0, "e4m3").T @ xq
    d_k1 = unpack_weight(d_words, d_scales)[np.arange(K)[:, None], runs(k1, K)]
    x_two = unpack_weight(x_words, x_scales)[:, unstriped(two)]
    d = 0.0625 * (d_k1.T @ x_two)
    z = f64(gn) * (0.75 * (y * d[:, unstriped(n2)] - (y[:, unstriped(n1)] * d)))
    h = mxq(f64(w2), 0, "e4m3").T @ mxq(z, 0, "e4m3")
    pa = h[:, unstriped(n3)]
    pb = h[:, unstriped(n4)]
    rb = np.maximum(pa, pb)
    ra = pa / (np.abs(pb) + 0.5)
    ds = np.zeros((N, S))
    ds[:, unstriped(n3)] = ra
    out = ds.copy()
    out[:, unstriped(n4)] = rb
    return out

@@ -1,0 +1,217 @@
+from contextlib import ExitStack
+
+import concourse.mybir as mybir
+
+K, T, S, N, H, G, W = 512, 2048, 512, 512, 512, 2048, 256
+FLOPS = 3 * 2 * 512 * 512 * 512
+
+F32 = mybir.dt.float32
+BF16 = mybir.dt.bfloat16
+I32 = mybir.dt.int32
+U32 = mybir.dt.uint32
+U16 = mybir.dt.uint16
+U8 = mybir.dt.uint8
+FP8X4 = mybir.dt.float8_e4m3fn_x4
+ALU = mybir.AluOpType
+ACT = mybir.ActivationFunctionType
+
+P = 128
+PACK = 4
+HALF = S // 2
+LIST_ROWS = 16
+
+
+def tile_picked_twkeycrossbratio_none_p_kernel(
+    tc, x_words, x_scales, w1, d_words, d_scales, gn, w2, offs, k1, two, n1, n2, n3, n4, out
+):
+    nc = tc.nc
+    with ExitStack() as ctx:
+        keep = ctx.enter_context(tc.tile_pool(name="keep", bufs=1))
+        ring = ctx.enter_context(tc.tile_pool(name="ring", bufs=4))
+        psum = ctx.enter_context(tc.psum_pool(name="psum", bufs=1))
+
+        slots = {"xt_words": "slot_a", "dk_scales": "slot_b"}
+
+        def load_list(name, source):
+            tile = keep.tile(list(source.shape), U16, name=name)
+            nc.sync.dma_start(tile[:], source)
+            return tile
+
+        def load_words(name, source):
+            tile = keep.tile([P, source.shape[2]], U32, name=name)
+            nc.sync.dma_start(tile[:].bitcast(I32), source[0].rearrange("p n t -> p (n t)").bitcast(I32))
+            return tile
+
+        def gather(name, table, offsets, dtype):
+            tile = keep.tile([P, S], dtype, name=name, tag=slots.get(name, name), align_bytes=64)
+            nc.vector.tensor_copy(tile[:], table[:].indirect(offsets[:]))
+            return tile
+
+        def quantize(name, grouped):
+            width = grouped[:].shape[1] // PACK
+            codes = keep.tile([P, width], U32, name=name + "_codes", align_bytes=64)
+            scales = keep.tile([P, width], U8, name=name + "_scales", tag=slots.get(name + "_scales", name + "_scales"), align_bytes=64)
+            nc.vector.quantize_mx(out=codes[:].bitcast(FP8X4), scales=scales[:], in_=grouped[:])
+            return codes, scales
+
+        def product(acc, lhs, cols, rhs):
+            nc.tensor.matmul_mx(
+                out=acc, lhsT=lhs[0][:, cols].bitcast(FP8X4), lhsT_scale=lhs[1][:, cols],
+                rhs=rhs[0][:].bitcast(FP8X4), rhs_scale=rhs[1][:], start=True, stop=True,
+            )
+
+        xs_table = keep.tile([P, T], U8, name="xs_table")
+        ds_table = keep.tile([P, G], U8, name="ds_table")
+        w1_rows = w1.rearrange("(p j) c -> p j c", j=PACK)
+        w1_raw = [keep.tile([P, PACK, H // 2], F32, name="w1_raw%d" % u) for u in range(2)]
+
+        offs_l = load_list("offs_l", offs)
+        xs_rows = x_scales[0].bitcast(I32)
+        for q in range(4):
+            nc.sync.dma_start(
+                xs_table[32 * q:32 * q + 32, :].bitcast(I32), xs_rows[4 * q:4 * q + 4, :].partition_broadcast(8)
+            )
+        nc.sync.dma_start(w1_raw[0][:], w1_rows[:, :, :H // 2])
+        k1_l = load_list("k1_l", k1)
+        ds_rows = d_scales[0].bitcast(I32)
+        nc.sync.dma_start(ds_table[:].bitcast(I32), ds_rows.unsqueeze(1).broadcast_to([16, 8, G // 4]))
+        nc.sync.dma_start(w1_raw[1][:], w1_rows[:, :, H // 2:])
+        xw_table = load_words("xw_table", x_words)
+        two_l = load_list("two_l", two)
+        gain_raw = keep.tile([P, PACK], F32, name="gain_raw")
+        nc.sync.dma_start(gain_raw[:], gn.rearrange("(p t) o -> p (t o)", t=PACK))
+        n1_l = load_list("n1_l", n1)
+        dw_table = load_words("dw_table", d_words)
+        n2_l = load_list("n2_l", n2)
+        n3_l = load_list("n3_l", n3)
+        n4_l = load_list("n4_l", n4)
+        gain = keep.tile([P, PACK], F32, name="gain")
+        nc.vector.tensor_scalar(gain[:], gain_raw[:], 0.75 * 0.0625, None, ALU.mult)
+
+        w1_grouped = keep.tile([P, PACK * H], BF16, name="w1_grouped", align_bytes=64)
+        w1_view = w1_grouped[:].rearrange("p (t m j) -> p m j t", t=PACK, j=PACK)
+        for u in range(2):
+            nc.scalar.copy(
+                w1_view[:, u * (P // 2):(u + 1) * (P // 2), :, :],
+                w1_raw[u][:].rearrange("p j (m t) -> p m j t", t=PACK),
+            )
+
+        xq_scales = gather("xq_scales", xs_table, offs_l, U8)
+        w1_q = quantize("w1", w1_grouped)
+        xq_words = gather("xq_words", xw_table, offs_l, U32)
+        y_sb, d_sb, d_acc = [], [], []
+        for t in range(PACK):
+            acc = psum.tile([P, S], F32, name="y_acc%d" % t, tag="left%d" % t)
+            product(acc[:], w1_q, slice(t * P, (t + 1) * P), (xq_words, xq_scales))
+            y_t = keep.tile([P, S], F32, name="y%d" % t)
+            nc.scalar.activation(y_t[:], acc[:], ACT.Copy, scale=gain[:, t:t + 1])
+            y_sb.append(y_t)
+
+        dk_scales = gather("dk_scales", ds_table, k1_l, U8)
+        dk_scales_dealt = keep.tile([P, H], U8, name="dk_scales_dealt", align_bytes=64)
+        nc.vector.tensor_copy(
+            dk_scales_dealt[:].rearrange("p (t m) -> p t m", t=PACK),
+            dk_scales[:].rearrange("p (m t) -> p t m", t=PACK),
+        )
+        for c in range(1, 4):
+            nc.sync.dma_start(
+                dk_scales_dealt[c:P:32, :].bitcast(I32), dk_scales_dealt[8 * c:P:32, :].bitcast(I32)
+            )
+        w2_raw = keep.tile([P, PACK, N], F32, name="w2_raw", tag="slot_b", align_bytes=64)
+        nc.sync.dma_start(w2_raw[:], w2.rearrange("(p j) c -> p j c", j=PACK))
+        xt_scales = gather("xt_scales", xs_table, two_l, U8)
+        xt_words = gather("xt_words", xw_table, two_l, U32)
+        dk_words = gather("dk_words", dw_table, k1_l, U32)
+        dk_words_dealt = keep.tile([P, H], U32, name="dk_words_dealt", align_bytes=64)
+        nc.vector.tensor_copy(
+            dk_words_dealt[:].rearrange("p (t m) -> p m t", t=PACK),
+            dk_words[:].rearrange("p (m t) -> p m t", t=PACK),
+        )
+        for t in range(PACK):
+            acc = psum.tile([P, S], F32, name="d_acc%d" % t, tag="right%d" % t)
+            product(acc[:], (dk_words_dealt, dk_scales_dealt), slice(t * P, (t + 1) * P), (xt_words, xt_scales))
+            d_t = keep.tile([P, S], F32, name="d%d" % t)
+            nc.scalar.copy(d_t[:], acc[:])
+            d_sb.append(d_t)
+            d_acc.append(acc)
+
+        h_sb = [keep.tile([P, S], F32, name="h%d" % m) for m in range(N // P)]
+        w2_grouped = keep.tile([P, PACK * N], BF16, name="w2_grouped", align_bytes=64)
+        nc.vector.tensor_copy(
+            w2_grouped[:].rearrange("p (c i j) -> p c j i", i=4, j=PACK),
+            w2_raw[:].rearrange("p j (c i) -> p c j i", i=4),
+        )
+        w2_q = quantize("w2", w2_grouped)
+        h_acc = []
+        for u in range(2):
+            cols = slice(u * HALF, (u + 1) * HALF)
+            lcols = slice(u * HALF // LIST_ROWS, (u + 1) * HALF // LIST_ROWS)
+            first = keep.tile([P, PACK, HALF], F32, name="first%d" % u)
+            second = keep.tile([P, PACK, HALF], F32, name="second%d" % u)
+            y_at = keep.tile([P, PACK, HALF], F32, name="y_at%d" % u, tag=("y_at0", "slot_a")[u], align_bytes=64)
+            on_scalar = range(0) if u == 0 else range(PACK)
+            for t in range(PACK):
+                nc.scalar.activation(y_at[:, t, :], y_sb[t][:].indirect(n1_l[:, lcols]), ACT.Copy)
+                nc.vector.tensor_tensor(second[:, t, :], y_at[:, t, :], d_acc[t][:, cols], ALU.mult)
+                if t not in on_scalar:
+                    nc.vector.tensor_tensor(first[:, t, :], d_sb[t][:].indirect(n2_l[:, lcols]), y_sb[t][:, cols], ALU.mult)
+            for t in on_scalar:
+                d_at = keep.tile([P, HALF], F32, name="d_at%d" % t)
+                nc.scalar.activation(d_at[:], d_sb[t][:].indirect(n2_l[:, lcols]), ACT.Copy)
+                nc.vector.tensor_tensor(first[:, t, :], d_at[:], y_sb[t][:, cols], ALU.mult)
+            for m, acc in enumerate(h_acc):
+                nc.scalar.copy(h_sb[m][:, :HALF], acc[:])
+            h_acc = []
+            z_grouped = keep.tile([P, PACK * HALF], BF16, name="z_grouped%d" % u, align_bytes=64)
+            nc.vector.tensor_tensor(
+                z_grouped[:].rearrange("p (c i t) -> p c t i", i=4, t=PACK),
+                first[:].rearrange("p t (c i) -> p c t i", i=4),
+                second[:].rearrange("p t (c i) -> p c t i", i=4),
+                ALU.subtract,
+            )
+            z_q = quantize("z%d" % u, z_grouped)
+            for m in range(N // P):
+                acc = psum.tile([P, HALF], F32, name="h_acc%d_%d" % (u, m), tag=("left%d", "right%d")[u] % m)
+                product(acc[:], w2_q, slice(m * P, (m + 1) * P), z_q)
+                h_acc.append(acc)
+        for m, acc in enumerate(h_acc):
+            nc.scalar.copy(h_sb[m][:, HALF:], acc[:])
+
+        blocks = range(N // P)
+        last = blocks[-1]
+        pa, inverse, larger, result = [], [], [], []
+
+        def put_larger(m):
+            nc.scalar.activation(result[m][:].indirect(n4_l[:]), larger[m][:], ACT.Copy)
+
+        def put_ratio(m):
+            nc.vector.tensor_tensor(result[m][:].indirect(n3_l[:]), pa[m][:], inverse[m][:], ALU.mult)
+
+        def store(m):
+            nc.sync.dma_start(out[m * P:(m + 1) * P, :], result[m][:])
+
+        for m in blocks:
+            pa.append(ring.tile([P, W], F32, name="pa"))
+            pb = ring.tile([P, W], F32, name="pb")
+            nc.vector.tensor_copy(pb[:], h_sb[m][:].indirect(n4_l[:]))
+            nc.vector.tensor_copy(pa[m][:], h_sb[m][:].indirect(n3_l[:]))
+            size = ring.tile([P, W], F32, name="size")
+            nc.scalar.activation(size[:], pb[:], ACT.Abs)
+            root = ring.tile([P, W], F32, name="root")
+            nc.scalar.activation(root[:], size[:], ACT.Abs_reciprocal_sqrt, bias=0.5)
+            inverse.append(ring.tile([P, W], F32, name="inverse"))
+            nc.scalar.activation(inverse[m][:], root[:], ACT.Square)
+            larger.append(ring.tile([P, W], F32, name="larger"))
+            nc.vector.tensor_tensor(larger[m][:], pa[m][:], pb[:], ALU.max)
+            result.append(ring.tile([P, S], F32, name="result"))
+            if m == 0:
+                put_larger(m)
+        put_ratio(0)
+        store(0)
+        put_ratio(last)
+        for m in blocks[1:last]:
+            put_larger(m)
+            put_ratio(m)
+            store(m)
+        put_larger(last)
+        store(last)

@@ -30,7 +30,7 @@ def tile_picked_twkeycrossbratio_none_p_kernel(
         ring = ctx.enter_context(tc.tile_pool(name="ring", bufs=4))
         psum = ctx.enter_context(tc.psum_pool(name="psum", bufs=1))
 
-        slots = {"xt_words": "slot_a", "dk_scales": "slot_b"}
+        slots = {"xt_words": "slot_a", "dk_scales": "slot_b", "dw_table": "slot_b"}
 
         def load_list(name, source):
             tile = keep.tile(list(source.shape), U16, name=name)
@@ -38,7 +38,7 @@ def tile_picked_twkeycrossbratio_none_p_kernel(
             return tile
 
         def load_words(name, source):
-            tile = keep.tile([P, source.shape[2]], U32, name=name)
+            tile = keep.tile([P, source.shape[2]], U32, name=name, tag=slots.get(name, name), align_bytes=64)
             nc.sync.dma_start(tile[:].bitcast(I32), source[0].rearrange("p n t -> p (n t)").bitcast(I32))
             return tile
 
@@ -63,30 +63,34 @@ def tile_picked_twkeycrossbratio_none_p_kernel(
         xs_table = keep.tile([P, T], U8, name="xs_table")
         ds_table = keep.tile([P, G], U8, name="ds_table")
         w1_rows = w1.rearrange("(p j) c -> p j c", j=PACK)
-        w1_raw = [keep.tile([P, PACK, H // 2], F32, name="w1_raw%d" % u) for u in range(2)]
+        w1_raw = [keep.tile([P, PACK, H // 2], F32, name="w1_raw%d" % u, tag="slot_w%d" % u) for u in range(2)]
 
+        k1_l = load_list("k1_l", k1)
+        ds_rows = d_scales[0].bitcast(I32)
+        nc.sync.dma_start(ds_table[:].bitcast(I32), ds_rows.unsqueeze(1).broadcast_to([16, 8, G // 4]))
         offs_l = load_list("offs_l", offs)
         xs_rows = x_scales[0].bitcast(I32)
         for q in range(4):
             nc.sync.dma_start(
                 xs_table[32 * q:32 * q + 32, :].bitcast(I32), xs_rows[4 * q:4 * q + 4, :].partition_broadcast(8)
             )
-        nc.sync.dma_start(w1_raw[0][:], w1_rows[:, :, :H // 2])
-        k1_l = load_list("k1_l", k1)
-        ds_rows = d_scales[0].bitcast(I32)
-        nc.sync.dma_start(ds_table[:].bitcast(I32), ds_rows.unsqueeze(1).broadcast_to([16, 8, G // 4]))
-        nc.sync.dma_start(w1_raw[1][:], w1_rows[:, :, H // 2:])
-        xw_table = load_words("xw_table", x_words)
+        for u in range(2):
+            nc.sync.dma_start(w1_raw[u][:], w1_rows[:, :, u * (H // 2):(u + 1) * (H // 2)])
         two_l = load_list("two_l", two)
         gain_raw = keep.tile([P, PACK], F32, name="gain_raw")
         nc.sync.dma_start(gain_raw[:], gn.rearrange("(p t) o -> p (t o)", t=PACK))
         n1_l = load_list("n1_l", n1)
-        dw_table = load_words("dw_table", d_words)
         n2_l = load_list("n2_l", n2)
+        xw_table = load_words("xw_table", x_words)
         n3_l = load_list("n3_l", n3)
         n4_l = load_list("n4_l", n4)
         gain = keep.tile([P, PACK], F32, name="gain")
         nc.vector.tensor_scalar(gain[:], gain_raw[:], 0.75 * 0.0625, None, ALU.mult)
+
+        warm_in = keep.tile([P, 1], F32, name="warm_in")
+        nc.gpsimd.memset(warm_in[:], 1.0)
+        warm_out = keep.tile([P, 1], F32, name="warm_out")
+        nc.scalar.activation(warm_out[:], warm_in[:], ACT.Abs_reciprocal_sqrt, bias=0.5)
 
         w1_grouped = keep.tile([P, PACK * H], BF16, name="w1_grouped", align_bytes=64)
         w1_view = w1_grouped[:].rearrange("p (t m j) -> p m j t", t=PACK, j=PACK)
@@ -96,6 +100,21 @@ def tile_picked_twkeycrossbratio_none_p_kernel(
                 w1_raw[u][:].rearrange("p j (m t) -> p m j t", t=PACK),
             )
 
+        dk_scales = gather("dk_scales", ds_table, k1_l, U8)
+        dk_scales_dealt = keep.tile([P, H], U8, name="dk_scales_dealt", align_bytes=64)
+        nc.vector.tensor_copy(
+            dk_scales_dealt[:].rearrange("p (t m) -> p t m", t=PACK),
+            dk_scales[:].rearrange("p (m t) -> p t m", t=PACK),
+        )
+        dk_plane = keep.tile([P, H], U8, name="dk_plane", align_bytes=64)
+        nc.gpsimd.memset(dk_plane[:].bitcast(I32), 0)
+        for q in range(4):
+            nc.sync.dma_start(
+                dk_plane[32 * q:32 * q + 4, :].bitcast(I32), dk_scales_dealt[32 * q:32 * q + 32:8, :].bitcast(I32)
+            )
+        dw_table = load_words("dw_table", d_words)
+        w2_raw = keep.tile([P, PACK, N], F32, name="w2_raw", tag="slot_w1")
+        nc.sync.dma_start(w2_raw[:], w2.rearrange("(p j) c -> p j c", j=PACK))
         xq_scales = gather("xq_scales", xs_table, offs_l, U8)
         w1_q = quantize("w1", w1_grouped)
         xq_words = gather("xq_words", xw_table, offs_l, U32)
@@ -107,36 +126,24 @@ def tile_picked_twkeycrossbratio_none_p_kernel(
             nc.scalar.activation(y_t[:], acc[:], ACT.Copy, scale=gain[:, t:t + 1])
             y_sb.append(y_t)
 
-        dk_scales = gather("dk_scales", ds_table, k1_l, U8)
-        dk_scales_dealt = keep.tile([P, H], U8, name="dk_scales_dealt", align_bytes=64)
-        nc.vector.tensor_copy(
-            dk_scales_dealt[:].rearrange("p (t m) -> p t m", t=PACK),
-            dk_scales[:].rearrange("p (m t) -> p t m", t=PACK),
-        )
-        for c in range(1, 4):
-            nc.sync.dma_start(
-                dk_scales_dealt[c:P:32, :].bitcast(I32), dk_scales_dealt[8 * c:P:32, :].bitcast(I32)
-            )
-        w2_raw = keep.tile([P, PACK, N], F32, name="w2_raw", tag="slot_b", align_bytes=64)
-        nc.sync.dma_start(w2_raw[:], w2.rearrange("(p j) c -> p j c", j=PACK))
         xt_scales = gather("xt_scales", xs_table, two_l, U8)
         xt_words = gather("xt_words", xw_table, two_l, U32)
         dk_words = gather("dk_words", dw_table, k1_l, U32)
-        dk_words_dealt = keep.tile([P, H], U32, name="dk_words_dealt", align_bytes=64)
+        dk_words_dealt = keep.tile([P, H], U32, name="dk_words_dealt", tag="slot_d", align_bytes=64)
         nc.vector.tensor_copy(
             dk_words_dealt[:].rearrange("p (t m) -> p m t", t=PACK),
             dk_words[:].rearrange("p (m t) -> p m t", t=PACK),
         )
         for t in range(PACK):
             acc = psum.tile([P, S], F32, name="d_acc%d" % t, tag="right%d" % t)
-            product(acc[:], (dk_words_dealt, dk_scales_dealt), slice(t * P, (t + 1) * P), (xt_words, xt_scales))
+            product(acc[:], (dk_words_dealt, dk_plane), slice(t * P, (t + 1) * P), (xt_words, xt_scales))
             d_t = keep.tile([P, S], F32, name="d%d" % t)
             nc.scalar.copy(d_t[:], acc[:])
             d_sb.append(d_t)
             d_acc.append(acc)
 
         h_sb = [keep.tile([P, S], F32, name="h%d" % m) for m in range(N // P)]
-        w2_grouped = keep.tile([P, PACK * N], BF16, name="w2_grouped", align_bytes=64)
+        w2_grouped = keep.tile([P, PACK * N], BF16, name="w2_grouped", tag="slot_g", align_bytes=64)
         nc.vector.tensor_copy(
             w2_grouped[:].rearrange("p (c i j) -> p c j i", i=4, j=PACK),
             w2_raw[:].rearrange("p j (c i) -> p c j i", i=4),
@@ -146,19 +153,25 @@ def tile_picked_twkeycrossbratio_none_p_kernel(
         for u in range(2):
             cols = slice(u * HALF, (u + 1) * HALF)
             lcols = slice(u * HALF // LIST_ROWS, (u + 1) * HALF // LIST_ROWS)
-            first = keep.tile([P, PACK, HALF], F32, name="first%d" % u)
-            second = keep.tile([P, PACK, HALF], F32, name="second%d" % u)
-            y_at = keep.tile([P, PACK, HALF], F32, name="y_at%d" % u, tag=("y_at0", "slot_a")[u], align_bytes=64)
+            first = keep.tile([P, PACK, HALF], F32, name="first%d" % u, tag=("slot_g", "first1")[u], align_bytes=64)
+            second = keep.tile([P, PACK, HALF], F32, name="second%d" % u, tag=("slot_w1", "second1")[u])
+            if u == 0:
+                early = keep.tile([P, 2, HALF], F32, name="early")
+                late = keep.tile([P, 2, HALF], F32, name="late", tag="slot_d", align_bytes=64)
+                y_at = [early[:, 0, :], early[:, 1, :], late[:, 0, :], late[:, 1, :]]
+            else:
+                held = keep.tile([P, 2 * PACK, HALF], F32, name="held", tag="slot_a", align_bytes=64)
+                y_at = [held[:, t, :] for t in range(PACK)]
             on_scalar = range(0) if u == 0 else range(PACK)
             for t in range(PACK):
-                nc.scalar.activation(y_at[:, t, :], y_sb[t][:].indirect(n1_l[:, lcols]), ACT.Copy)
-                nc.vector.tensor_tensor(second[:, t, :], y_at[:, t, :], d_acc[t][:, cols], ALU.mult)
+                nc.scalar.activation(y_at[t], y_sb[t][:].indirect(n1_l[:, lcols]), ACT.Copy)
+                nc.vector.tensor_tensor(second[:, t, :], y_at[t], d_acc[t][:, cols], ALU.mult)
                 if t not in on_scalar:
                     nc.vector.tensor_tensor(first[:, t, :], d_sb[t][:].indirect(n2_l[:, lcols]), y_sb[t][:, cols], ALU.mult)
             for t in on_scalar:
-                d_at = keep.tile([P, HALF], F32, name="d_at%d" % t)
-                nc.scalar.activation(d_at[:], d_sb[t][:].indirect(n2_l[:, lcols]), ACT.Copy)
-                nc.vector.tensor_tensor(first[:, t, :], d_at[:], y_sb[t][:, cols], ALU.mult)
+                d_at = held[:, PACK + t, :]
+                nc.scalar.activation(d_at, d_sb[t][:].indirect(n2_l[:, lcols]), ACT.Copy)
+                nc.vector.tensor_tensor(first[:, t, :], d_at, y_sb[t][:, cols], ALU.mult)
             for m, acc in enumerate(h_acc):
                 nc.scalar.copy(h_sb[m][:, :HALF], acc[:])
             h_acc = []

from contextlib import ExitStack

import concourse.mybir as mybir

K, T, S, N, H, G, W = 512, 2048, 512, 512, 512, 2048, 256
FLOPS = 3 * 2 * 512 * 512 * 512

F32 = mybir.dt.float32
BF16 = mybir.dt.bfloat16
I32 = mybir.dt.int32
U32 = mybir.dt.uint32
U16 = mybir.dt.uint16
U8 = mybir.dt.uint8
FP8X4 = mybir.dt.float8_e4m3fn_x4
ALU = mybir.AluOpType
ACT = mybir.ActivationFunctionType

P = 128
PACK = 4
HALF = S // 2
LIST_ROWS = 16


def tile_picked_twkeycrossbratio_none_p_kernel(
    tc, x_words, x_scales, w1, d_words, d_scales, gn, w2, offs, k1, two, n1, n2, n3, n4, out
):
    nc = tc.nc
    with ExitStack() as ctx:
        keep = ctx.enter_context(tc.tile_pool(name="keep", bufs=1))
        ring = ctx.enter_context(tc.tile_pool(name="ring", bufs=4))
        psum = ctx.enter_context(tc.psum_pool(name="psum", bufs=1))

        slots = {"xt_words": "slot_a", "dk_scales": "slot_b", "dw_table": "slot_b"}

        def load_list(name, source):
            tile = keep.tile(list(source.shape), U16, name=name)
            nc.sync.dma_start(tile[:], source)
            return tile

        def load_words(name, source):
            tile = keep.tile([P, source.shape[2]], U32, name=name, tag=slots.get(name, name), align_bytes=64)
            nc.sync.dma_start(tile[:].bitcast(I32), source[0].rearrange("p n t -> p (n t)").bitcast(I32))
            return tile

        def gather(name, table, offsets, dtype):
            tile = keep.tile([P, S], dtype, name=name, tag=slots.get(name, name), align_bytes=64)
            nc.vector.tensor_copy(tile[:], table[:].indirect(offsets[:]))
            return tile

        def quantize(name, grouped):
            width = grouped[:].shape[1] // PACK
            codes = keep.tile([P, width], U32, name=name + "_codes", align_bytes=64)
            scales = keep.tile([P, width], U8, name=name + "_scales", tag=slots.get(name + "_scales", name + "_scales"), align_bytes=64)
            nc.vector.quantize_mx(out=codes[:].bitcast(FP8X4), scales=scales[:], in_=grouped[:])
            return codes, scales

        def product(acc, lhs, cols, rhs):
            nc.tensor.matmul_mx(
                out=acc, lhsT=lhs[0][:, cols].bitcast(FP8X4), lhsT_scale=lhs[1][:, cols],
                rhs=rhs[0][:].bitcast(FP8X4), rhs_scale=rhs[1][:], start=True, stop=True,
            )

        xs_table = keep.tile([P, T], U8, name="xs_table")
        ds_table = keep.tile([P, G], U8, name="ds_table")
        w1_rows = w1.rearrange("(p j) c -> p j c", j=PACK)
        w1_raw = [keep.tile([P, PACK, H // 2], F32, name="w1_raw%d" % u, tag="slot_w%d" % u) for u in range(2)]

        k1_l = load_list("k1_l", k1)
        ds_rows = d_scales[0].bitcast(I32)
        nc.sync.dma_start(ds_table[:].bitcast(I32), ds_rows.unsqueeze(1).broadcast_to([16, 8, G // 4]))
        offs_l = load_list("offs_l", offs)
        xs_rows = x_scales[0].bitcast(I32)
        for q in range(4):
            nc.sync.dma_start(
                xs_table[32 * q:32 * q + 32, :].bitcast(I32), xs_rows[4 * q:4 * q + 4, :].partition_broadcast(8)
            )
        for u in range(2):
            nc.sync.dma_start(w1_raw[u][:], w1_rows[:, :, u * (H // 2):(u + 1) * (H // 2)])
        two_l = load_list("two_l", two)
        gain_raw = keep.tile([P, PACK], F32, name="gain_raw")
        nc.sync.dma_start(gain_raw[:], gn.rearrange("(p t) o -> p (t o)", t=PACK))
        n1_l = load_list("n1_l", n1)
        n2_l = load_list("n2_l", n2)
        xw_table = load_words("xw_table", x_words)
        n3_l = load_list("n3_l", n3)
        n4_l = load_list("n4_l", n4)
        gain = keep.tile([P, PACK], F32, name="gain")
        nc.vector.tensor_scalar(gain[:], gain_raw[:], 0.75 * 0.0625, None, ALU.mult)

        warm_in = keep.tile([P, 1], F32, name="warm_in")
        nc.gpsimd.memset(warm_in[:], 1.0)
        warm_out = keep.tile([P, 1], F32, name="warm_out")
        nc.scalar.activation(warm_out[:], warm_in[:], ACT.Abs_reciprocal_sqrt, bias=0.5)

        w1_grouped = keep.tile([P, PACK * H], BF16, name="w1_grouped", align_bytes=64)
        w1_view = w1_grouped[:].rearrange("p (t m j) -> p m j t", t=PACK, j=PACK)
        for u in range(2):
            nc.scalar.copy(
                w1_view[:, u * (P // 2):(u + 1) * (P // 2), :, :],
                w1_raw[u][:].rearrange("p j (m t) -> p m j t", t=PACK),
            )

        dk_scales = gather("dk_scales", ds_table, k1_l, U8)
        dk_scales_dealt = keep.tile([P, H], U8, name="dk_scales_dealt", align_bytes=64)
        nc.vector.tensor_copy(
            dk_scales_dealt[:].rearrange("p (t m) -> p t m", t=PACK),
            dk_scales[:].rearrange("p (m t) -> p t m", t=PACK),
        )
        dk_plane = keep.tile([P, H], U8, name="dk_plane", align_bytes=64)
        nc.gpsimd.memset(dk_plane[:].bitcast(I32), 0)
        for q in range(4):
            nc.sync.dma_start(
                dk_plane[32 * q:32 * q + 4, :].bitcast(I32), dk_scales_dealt[32 * q:32 * q + 32:8, :].bitcast(I32)
            )
        dw_table = load_words("dw_table", d_words)
        w2_raw = keep.tile([P, PACK, N], F32, name="w2_raw", tag="slot_w1")
        nc.sync.dma_start(w2_raw[:], w2.rearrange("(p j) c -> p j c", j=PACK))
        xq_scales = gather("xq_scales", xs_table, offs_l, U8)
        w1_q = quantize("w1", w1_grouped)
        xq_words = gather("xq_words", xw_table, offs_l, U32)
        y_sb, d_sb, d_acc = [], [], []
        for t in range(PACK):
            acc = psum.tile([P, S], F32, name="y_acc%d" % t, tag="left%d" % t)
            product(acc[:], w1_q, slice(t * P, (t + 1) * P), (xq_words, xq_scales))
            y_t = keep.tile([P, S], F32, name="y%d" % t)
            nc.scalar.activation(y_t[:], acc[:], ACT.Copy, scale=gain[:, t:t + 1])
            y_sb.append(y_t)

        xt_scales = gather("xt_scales", xs_table, two_l, U8)
        xt_words = gather("xt_words", xw_table, two_l, U32)
        dk_words = gather("dk_words", dw_table, k1_l, U32)
        dk_words_dealt = keep.tile([P, H], U32, name="dk_words_dealt", tag="slot_d", align_bytes=64)
        nc.vector.tensor_copy(
            dk_words_dealt[:].rearrange("p (t m) -> p m t", t=PACK),
            dk_words[:].rearrange("p (m t) -> p m t", t=PACK),
        )
        for t in range(PACK):
            acc = psum.tile([P, S], F32, name="d_acc%d" % t, tag="right%d" % t)
            product(acc[:], (dk_words_dealt, dk_plane), slice(t * P, (t + 1) * P), (xt_words, xt_scales))
            d_t = keep.tile([P, S], F32, name="d%d" % t)
            nc.scalar.copy(d_t[:], acc[:])
            d_sb.append(d_t)
            d_acc.append(acc)

        h_sb = [keep.tile([P, S], F32, name="h%d" % m) for m in range(N // P)]
        w2_grouped = keep.tile([P, PACK * N], BF16, name="w2_grouped", tag="slot_g", align_bytes=64)
        nc.vector.tensor_copy(
            w2_grouped[:].rearrange("p (c i j) -> p c j i", i=4, j=PACK),
            w2_raw[:].rearrange("p j (c i) -> p c j i", i=4),
        )
        w2_q = quantize("w2", w2_grouped)
        h_acc = []
        for u in range(2):
            cols = slice(u * HALF, (u + 1) * HALF)
            lcols = slice(u * HALF // LIST_ROWS, (u + 1) * HALF // LIST_ROWS)
            first = keep.tile([P, PACK, HALF], F32, name="first%d" % u, tag=("slot_g", "first1")[u], align_bytes=64)
            second = keep.tile([P, PACK, HALF], F32, name="second%d" % u, tag=("slot_w1", "second1")[u])
            if u == 0:
                early = keep.tile([P, 2, HALF], F32, name="early")
                late = keep.tile([P, 2, HALF], F32, name="late", tag="slot_d", align_bytes=64)
                y_at = [early[:, 0, :], early[:, 1, :], late[:, 0, :], late[:, 1, :]]
            else:
                held = keep.tile([P, 2 * PACK, HALF], F32, name="held", tag="slot_a", align_bytes=64)
                y_at = [held[:, t, :] for t in range(PACK)]
            on_scalar = range(0) if u == 0 else range(PACK)
            for t in range(PACK):
                nc.scalar.activation(y_at[t], y_sb[t][:].indirect(n1_l[:, lcols]), ACT.Copy)
                nc.vector.tensor_tensor(second[:, t, :], y_at[t], d_acc[t][:, cols], ALU.mult)
                if t not in on_scalar:
                    nc.vector.tensor_tensor(first[:, t, :], d_sb[t][:].indirect(n2_l[:, lcols]), y_sb[t][:, cols], ALU.mult)
            for t in on_scalar:
                d_at = held[:, PACK + t, :]
                nc.scalar.activation(d_at, d_sb[t][:].indirect(n2_l[:, lcols]), ACT.Copy)
                nc.vector.tensor_tensor(first[:, t, :], d_at, y_sb[t][:, cols], ALU.mult)
            for m, acc in enumerate(h_acc):
                nc.scalar.copy(h_sb[m][:, :HALF], acc[:])
            h_acc = []
            z_grouped = keep.tile([P, PACK * HALF], BF16, name="z_grouped%d" % u, align_bytes=64)
            nc.vector.tensor_tensor(
                z_grouped[:].rearrange("p (c i t) -> p c t i", i=4, t=PACK),
                first[:].rearrange("p t (c i) -> p c t i", i=4),
                second[:].rearrange("p t (c i) -> p c t i", i=4),
                ALU.subtract,
            )
            z_q = quantize("z%d" % u, z_grouped)
            for m in range(N // P):
                acc = psum.tile([P, HALF], F32, name="h_acc%d_%d" % (u, m), tag=("left%d", "right%d")[u] % m)
                product(acc[:], w2_q, slice(m * P, (m + 1) * P), z_q)
                h_acc.append(acc)
        for m, acc in enumerate(h_acc):
            nc.scalar.copy(h_sb[m][:, HALF:], acc[:])

        blocks = range(N // P)
        last = blocks[-1]
        pa, inverse, larger, result = [], [], [], []

        def put_larger(m):
            nc.scalar.activation(result[m][:].indirect(n4_l[:]), larger[m][:], ACT.Copy)

        def put_ratio(m):
            nc.vector.tensor_tensor(result[m][:].indirect(n3_l[:]), pa[m][:], inverse[m][:], ALU.mult)

        def store(m):
            nc.sync.dma_start(out[m * P:(m + 1) * P, :], result[m][:])

        for m in blocks:
            pa.append(ring.tile([P, W], F32, name="pa"))
            pb = ring.tile([P, W], F32, name="pb")
            nc.vector.tensor_copy(pb[:], h_sb[m][:].indirect(n4_l[:]))
            nc.vector.tensor_copy(pa[m][:], h_sb[m][:].indirect(n3_l[:]))
            size = ring.tile([P, W], F32, name="size")
            nc.scalar.activation(size[:], pb[:], ACT.Abs)
            root = ring.tile([P, W], F32, name="root")
            nc.scalar.activation(root[:], size[:], ACT.Abs_reciprocal_sqrt, bias=0.5)
            inverse.append(ring.tile([P, W], F32, name="inverse"))
            nc.scalar.activation(inverse[m][:], root[:], ACT.Square)
            larger.append(ring.tile([P, W], F32, name="larger"))
            nc.vector.tensor_tensor(larger[m][:], pa[m][:], pb[:], ALU.max)
            result.append(ring.tile([P, S], F32, name="result"))
            if m == 0:
                put_larger(m)
        put_ratio(0)
        store(0)
        put_ratio(last)
        for m in blocks[1:last]:
            put_larger(m)
            put_ratio(m)
            store(m)
        put_larger(last)
        store(last)
